import numpy as np
import ml_dtypes

BF16 = ml_dtypes.bfloat16


def bf(x):
    return np.asarray(x, np.float32).astype(BF16)


def f32(x):
    return np.asarray(x, np.float32)


def f64(x):
    return np.asarray(x).astype(np.float64)


def striped(idx):
    return np.tile(idx.reshape(-1, 16).T, (8, 1))


S, K, M, N, E, Q = 512, 256, 128, 384, 4, 96


def setup_inputs():
    return {"base": bf(np.random.standard_normal((M, S))), "x": bf(np.random.standard_normal((K, N))), "w": bf(np.random.standard_normal((E, K, M)) / np.sqrt(K)), "b": f32(0.5 * np.random.standard_normal((M, 1))), "offs": striped(np.random.permutation(S)[:N])}


def reference(base, x, w, b, offs):
    idx = offs[:16].T.reshape(-1)
    z = f64(base).copy()
    for e in range(E):
        z[:, idx[e * Q : (e + 1) * Q]] += f64(w)[e].T @ f64(x)[:, e * Q : (e + 1) * Q]
    return z + f64(b)

@@ -1,0 +1,57 @@
+import concourse.mybir as mybir
+from concourse.masks import make_identity
+
+P = 128
+S = 512
+K = 256
+N = 384
+E = 4
+Q = N // E
+KB = K // P
+QC = Q // 16
+
+FLOPS = 2 * K * P * N
+
+BF16, F32, U16 = mybir.dt.bfloat16, mybir.dt.float32, mybir.dt.uint16
+
+
+def tile_scatter_matmul_kernel(tc, base, x, w, b, offs, out):
+    nc = tc.nc
+    with (
+        tc.tile_pool(name="held", bufs=1) as held,
+        tc.psum_pool(name="psum", bufs=1) as psum,
+    ):
+        offsets = held.tile([P, N // 16], U16, name="offsets")
+        nc.sync.dma_start(offsets[:], offs)
+
+        ident = held.tile([P, P], BF16, name="ident")
+        make_identity(nc, ident[:])
+
+        base_tile = held.tile([P, S], BF16, name="base_tile")
+        nc.scalar.dma_start(base_tile[:], base)
+
+        x_tile = held.tile([P, KB, N], BF16, name="x_tile")
+        nc.sync.dma_start(x_tile[:], x.rearrange("(a p) n -> p a n", p=P))
+        w_tile = held.tile([P, E * KB, P], BF16, name="w_tile")
+        nc.scalar.dma_start(w_tile[:], w.rearrange("e (a p) m -> p (e a) m", p=P))
+
+        bias = held.tile([P, 1], F32, name="bias")
+        nc.gpsimd.dma_start(bias[:], b)
+
+        window = psum.tile([P, S], F32, name="window")
+        nc.tensor.matmul(window[:], ident[:], base_tile[:], start=True, stop=False)
+
+        for e in range(E):
+            places = window[:].indirect(offsets[:, e * QC : (e + 1) * QC])
+            for a in range(KB):
+                nc.tensor.matmul(
+                    places,
+                    w_tile[:, e * KB + a, :],
+                    x_tile[:, a, e * Q : (e + 1) * Q],
+                    start=False,
+                    stop=(e == E - 1 and a == KB - 1),
+                )
+
+        result = held.tile([P, S], F32, name="result")
+        nc.vector.tensor_scalar_add(result[:], window[:], bias[:])
+        nc.sync.dma_start(out, result[:])

@@ -31,12 +31,17 @@ def tile_scatter_matmul_kernel(tc, base, x, w, b, offs, out):
         nc.scalar.dma_start(base_tile[:], base)
 
         x_tile = held.tile([P, KB, N], BF16, name="x_tile")
-        nc.sync.dma_start(x_tile[:], x.rearrange("(a p) n -> p a n", p=P))
-        w_tile = held.tile([P, E * KB, P], BF16, name="w_tile")
-        nc.scalar.dma_start(w_tile[:], w.rearrange("e (a p) m -> p (e a) m", p=P))
+        nc.sync.dma_start(x_tile[:], x.rearrange("(p a) n -> p a n", a=KB))
+
+        w_tiles = []
+        for e in range(E):
+            w_tile = held.tile([P, KB, P], BF16, name="w_tile%d" % e)
+            queue = nc.scalar if e % 2 == 0 else nc.sync
+            queue.dma_start(w_tile[:], w[e].rearrange("(p a) m -> p a m", a=KB))
+            w_tiles.append(w_tile)
 
         bias = held.tile([P, 1], F32, name="bias")
-        nc.gpsimd.dma_start(bias[:], b)
+        nc.scalar.dma_start(bias[:], b)
 
         window = psum.tile([P, S], F32, name="window")
         nc.tensor.matmul(window[:], ident[:], base_tile[:], start=True, stop=False)
@@ -46,7 +51,7 @@ def tile_scatter_matmul_kernel(tc, base, x, w, b, offs, out):
             for a in range(KB):
                 nc.tensor.matmul(
                     places,
-                    w_tile[:, e * KB + a, :],
+                    w_tiles[e][:, a, :],
                     x_tile[:, a, e * Q : (e + 1) * Q],
                     start=False,
                     stop=(e == E - 1 and a == KB - 1),

@@ -10,6 +10,9 @@ Q = N // E
 KB = K // P
 QC = Q // 16
 
+WARM_UPS = 6
+WARM_COLS = 256
+
 FLOPS = 2 * K * P * N
 
 BF16, F32, U16 = mybir.dt.bfloat16, mybir.dt.float32, mybir.dt.uint16
@@ -23,6 +26,12 @@ def tile_scatter_matmul_kernel(tc, base, x, w, b, offs, out):
     ):
         offsets = held.tile([P, N // 16], U16, name="offsets")
         nc.sync.dma_start(offsets[:], offs)
+
+        zeros = held.tile([P, WARM_COLS], BF16, name="zeros")
+        nc.gpsimd.memset(zeros[:], 0.0)
+        unread = psum.tile([P, WARM_COLS], F32, name="unread")
+        for i in range(WARM_UPS):
+            nc.tensor.matmul(unread[:], zeros[:, 0:P], zeros[:], start=True, stop=True)
 
         ident = held.tile([P, P], BF16, name="ident")
         make_identity(nc, ident[:])

@@ -10,7 +10,7 @@ Q = N // E
 KB = K // P
 QC = Q // 16
 
-WARM_UPS = 6
+WARM_UPS = 8
 WARM_COLS = 256
 
 FLOPS = 2 * K * P * N

@@ -26,6 +26,8 @@ def tile_scatter_matmul_kernel(tc, base, x, w, b, offs, out):
     ):
         offsets = held.tile([P, N // 16], U16, name="offsets")
         nc.sync.dma_start(offsets[:], offs)
+        bias = held.tile([P, 1], F32, name="bias")
+        nc.sync.dma_start(bias[:], b)
 
         zeros = held.tile([P, WARM_COLS], BF16, name="zeros")
         nc.gpsimd.memset(zeros[:], 0.0)
@@ -40,17 +42,13 @@ def tile_scatter_matmul_kernel(tc, base, x, w, b, offs, out):
         nc.scalar.dma_start(base_tile[:], base)
 
         x_tile = held.tile([P, KB, N], BF16, name="x_tile")
-        nc.sync.dma_start(x_tile[:], x.rearrange("(p a) n -> p a n", a=KB))
+        nc.scalar.dma_start(x_tile[:], x.rearrange("(p a) n -> p a n", a=KB))
 
         w_tiles = []
         for e in range(E):
             w_tile = held.tile([P, KB, P], BF16, name="w_tile%d" % e)
-            queue = nc.scalar if e % 2 == 0 else nc.sync
-            queue.dma_start(w_tile[:], w[e].rearrange("(p a) m -> p a m", a=KB))
+            nc.scalar.dma_start(w_tile[:], w[e].rearrange("(p a) m -> p a m", a=KB))
             w_tiles.append(w_tile)
-
-        bias = held.tile([P, 1], F32, name="bias")
-        nc.scalar.dma_start(bias[:], b)
 
         window = psum.tile([P, S], F32, name="window")
         nc.tensor.matmul(window[:], ident[:], base_tile[:], start=True, stop=False)

@@ -12,6 +12,7 @@ QC = Q // 16
 
 WARM_UPS = 8
 WARM_COLS = 256
+HALVES = 2
 
 FLOPS = 2 * K * P * N
 
@@ -64,6 +65,8 @@ def tile_scatter_matmul_kernel(tc, base, x, w, b, offs, out):
                     stop=(e == E - 1 and a == KB - 1),
                 )
 
-        result = held.tile([P, S], F32, name="result")
-        nc.vector.tensor_scalar_add(result[:], window[:], bias[:])
-        nc.sync.dma_start(out, result[:])
+        for h in range(HALVES):
+            cols = slice(h * S // HALVES, (h + 1) * S // HALVES)
+            result = held.tile([P, S // HALVES], F32, name="result%d" % h)
+            nc.vector.tensor_scalar_add(result[:], window[:, cols], bias[:])
+            nc.sync.dma_start(out[:, cols], result[:])

@@ -9,6 +9,8 @@ E = 4
 Q = N // E
 KB = K // P
 QC = Q // 16
+EARLY = E // 2
+HEAD = (KB - 1) * N + EARLY * Q
 
 WARM_UPS = 8
 WARM_COLS = 256
@@ -42,11 +44,15 @@ def tile_scatter_matmul_kernel(tc, base, x, w, b, offs, out):
         base_tile = held.tile([P, S], BF16, name="base_tile")
         nc.scalar.dma_start(base_tile[:], base)
 
-        x_tile = held.tile([P, KB, N], BF16, name="x_tile")
-        nc.scalar.dma_start(x_tile[:], x.rearrange("(p a) n -> p a n", a=KB))
+        x_runs = x.rearrange("(p a) n -> p (a n)", a=KB)
+        x_head = held.tile([P, HEAD], BF16, name="x_head")
+        x_tail = held.tile([P, KB * N - HEAD], BF16, name="x_tail")
+        nc.scalar.dma_start(x_head[:], x_runs[:, 0:HEAD])
 
         w_tiles = []
         for e in range(E):
+            if e == EARLY:
+                nc.scalar.dma_start(x_tail[:], x_runs[:, HEAD : KB * N])
             w_tile = held.tile([P, KB, P], BF16, name="w_tile%d" % e)
             nc.scalar.dma_start(w_tile[:], w[e].rearrange("(p a) m -> p a m", a=KB))
             w_tiles.append(w_tile)
@@ -57,10 +63,15 @@ def tile_scatter_matmul_kernel(tc, base, x, w, b, offs, out):
         for e in range(E):
             places = window[:].indirect(offsets[:, e * QC : (e + 1) * QC])
             for a in range(KB):
+                first = a * N + e * Q
+                if first < HEAD:
+                    moving = x_head[:, first : first + Q]
+                else:
+                    moving = x_tail[:, first - HEAD : first - HEAD + Q]
                 nc.tensor.matmul(
                     places,
                     w_tiles[e][:, a, :],
-                    x_tile[:, a, e * Q : (e + 1) * Q],
+                    moving,
                     start=False,
                     stop=(e == E - 1 and a == KB - 1),
                 )

@@ -9,7 +9,7 @@ E = 4
 Q = N // E
 KB = K // P
 QC = Q // 16
-EARLY = E // 2
+EARLY = 1
 HEAD = (KB - 1) * N + EARLY * Q
 
 WARM_UPS = 8
@@ -51,11 +51,11 @@ def tile_scatter_matmul_kernel(tc, base, x, w, b, offs, out):
 
         w_tiles = []
         for e in range(E):
-            if e == EARLY:
-                nc.scalar.dma_start(x_tail[:], x_runs[:, HEAD : KB * N])
             w_tile = held.tile([P, KB, P], BF16, name="w_tile%d" % e)
             nc.scalar.dma_start(w_tile[:], w[e].rearrange("(p a) m -> p a m", a=KB))
             w_tiles.append(w_tile)
+            if e == EARLY:
+                nc.scalar.dma_start(x_tail[:], x_runs[:, HEAD : KB * N])
 
         window = psum.tile([P, S], F32, name="window")
         nc.tensor.matmul(window[:], ident[:], base_tile[:], start=True, stop=False)

@@ -12,8 +12,8 @@ QC = Q // 16
 EARLY = 1
 HEAD = (KB - 1) * N + EARLY * Q
 
-WARM_UPS = 8
-WARM_COLS = 256
+WARM_UPS = 16
+WARM_COLS = 128
 HALVES = 2
 
 FLOPS = 2 * K * P * N

@@ -9,7 +9,7 @@ E = 4
 Q = N // E
 KB = K // P
 QC = Q // 16
-EARLY = 1
+EARLY = 3
 HEAD = (KB - 1) * N + EARLY * Q
 
 WARM_UPS = 16
@@ -45,9 +45,8 @@ def tile_scatter_matmul_kernel(tc, base, x, w, b, offs, out):
         nc.scalar.dma_start(base_tile[:], base)
 
         x_runs = x.rearrange("(p a) n -> p (a n)", a=KB)
-        x_head = held.tile([P, HEAD], BF16, name="x_head")
-        x_tail = held.tile([P, KB * N - HEAD], BF16, name="x_tail")
-        nc.scalar.dma_start(x_head[:], x_runs[:, 0:HEAD])
+        x_tile = held.tile([P, KB * N], BF16, name="x_tile")
+        nc.scalar.dma_start(x_tile[:, 0:HEAD], x_runs[:, 0:HEAD])
 
         w_tiles = []
         for e in range(E):
@@ -55,7 +54,7 @@ def tile_scatter_matmul_kernel(tc, base, x, w, b, offs, out):
             nc.scalar.dma_start(w_tile[:], w[e].rearrange("(p a) m -> p a m", a=KB))
             w_tiles.append(w_tile)
             if e == EARLY:
-                nc.scalar.dma_start(x_tail[:], x_runs[:, HEAD : KB * N])
+                nc.scalar.dma_start(x_tile[:, HEAD : KB * N], x_runs[:, HEAD : KB * N])
 
         window = psum.tile([P, S], F32, name="window")
         nc.tensor.matmul(window[:], ident[:], base_tile[:], start=True, stop=False)
@@ -64,14 +63,10 @@ def tile_scatter_matmul_kernel(tc, base, x, w, b, offs, out):
             places = window[:].indirect(offsets[:, e * QC : (e + 1) * QC])
             for a in range(KB):
                 first = a * N + e * Q
-                if first < HEAD:
-                    moving = x_head[:, first : first + Q]
-                else:
-                    moving = x_tail[:, first - HEAD : first - HEAD + Q]
                 nc.tensor.matmul(
                     places,
                     w_tiles[e][:, a, :],
-                    moving,
+                    x_tile[:, first : first + Q],
                     start=False,
                     stop=(e == E - 1 and a == KB - 1),
                 )

@@ -9,8 +9,8 @@ E = 4
 Q = N // E
 KB = K // P
 QC = Q // 16
-EARLY = 3
-HEAD = (KB - 1) * N + EARLY * Q
+HEAD = 512
+EARLY = (HEAD - (KB - 1) * N) // Q
 
 WARM_UPS = 16
 WARM_COLS = 128

@@ -15,6 +15,7 @@ EARLY = (HEAD - (KB - 1) * N) // Q
 WARM_UPS = 16
 WARM_COLS = 128
 HALVES = 2
+ALIGN = 1024
 
 FLOPS = 2 * K * P * N
 
@@ -41,16 +42,16 @@ def tile_scatter_matmul_kernel(tc, base, x, w, b, offs, out):
         ident = held.tile([P, P], BF16, name="ident")
         make_identity(nc, ident[:])
 
-        base_tile = held.tile([P, S], BF16, name="base_tile")
+        base_tile = held.tile([P, S], BF16, name="base_tile", align_bytes=ALIGN)
         nc.scalar.dma_start(base_tile[:], base)
 
         x_runs = x.rearrange("(p a) n -> p (a n)", a=KB)
-        x_tile = held.tile([P, KB * N], BF16, name="x_tile")
+        x_tile = held.tile([P, KB * N], BF16, name="x_tile", align_bytes=ALIGN)
         nc.scalar.dma_start(x_tile[:, 0:HEAD], x_runs[:, 0:HEAD])
 
         w_tiles = []
         for e in range(E):
-            w_tile = held.tile([P, KB, P], BF16, name="w_tile%d" % e)
+            w_tile = held.tile([P, KB, P], BF16, name="w_tile%d" % e, align_bytes=ALIGN)
             nc.scalar.dma_start(w_tile[:], w[e].rearrange("(p a) m -> p a m", a=KB))
             w_tiles.append(w_tile)
             if e == EARLY:
@@ -73,6 +74,6 @@ def tile_scatter_matmul_kernel(tc, base, x, w, b, offs, out):
 
         for h in range(HALVES):
             cols = slice(h * S // HALVES, (h + 1) * S // HALVES)
-            result = held.tile([P, S // HALVES], F32, name="result%d" % h)
+            result = held.tile([P, S // HALVES], F32, name="result%d" % h, align_bytes=ALIGN)
             nc.vector.tensor_scalar_add(result[:], window[:, cols], bias[:])
             nc.sync.dma_start(out[:, cols], result[:])

@@ -15,7 +15,7 @@ EARLY = (HEAD - (KB - 1) * N) // Q
 WARM_UPS = 16
 WARM_COLS = 128
 HALVES = 2
-ALIGN = 1024
+ALIGN = 256
 
 FLOPS = 2 * K * P * N
 

@@ -12,7 +12,7 @@ QC = Q // 16
 HEAD = 512
 EARLY = (HEAD - (KB - 1) * N) // Q
 
-WARM_UPS = 16
+WARM_UPS = 10
 WARM_COLS = 128
 HALVES = 2
 ALIGN = 256

@@ -12,8 +12,9 @@ QC = Q // 16
 HEAD = 512
 EARLY = (HEAD - (KB - 1) * N) // Q
 
-WARM_UPS = 10
-WARM_COLS = 128
+WARM_UPS = 3
+WARM_COLS = 512
+ZERO_COLS = 16
 HALVES = 2
 ALIGN = 256
 
@@ -33,11 +34,17 @@ def tile_scatter_matmul_kernel(tc, base, x, w, b, offs, out):
         bias = held.tile([P, 1], F32, name="bias")
         nc.sync.dma_start(bias[:], b)
 
-        zeros = held.tile([P, WARM_COLS], BF16, name="zeros")
+        zeros = held.tile([P, ZERO_COLS], BF16, name="zeros")
         nc.gpsimd.memset(zeros[:], 0.0)
         unread = psum.tile([P, WARM_COLS], F32, name="unread")
         for i in range(WARM_UPS):
-            nc.tensor.matmul(unread[:], zeros[:, 0:P], zeros[:], start=True, stop=True)
+            nc.tensor.matmul(
+                unread[:],
+                zeros[:, 0:1].to_broadcast([P, P]),
+                zeros[:, 0:1].to_broadcast([P, WARM_COLS]),
+                start=True,
+                stop=True,
+            )
 
         ident = held.tile([P, P], BF16, name="ident")
         make_identity(nc, ident[:])

@@ -16,6 +16,7 @@ WARM_UPS = 3
 WARM_COLS = 512
 ZERO_COLS = 16
 HALVES = 2
+PROBE_COLS = 256
 ALIGN = 256
 
 FLOPS = 2 * K * P * N
@@ -66,6 +67,14 @@ def tile_scatter_matmul_kernel(tc, base, x, w, b, offs, out):
 
         window = psum.tile([P, S], F32, name="window")
         nc.tensor.matmul(window[:], ident[:], base_tile[:], start=True, stop=False)
+
+        nc.tensor.matmul(
+            unread[:, 0:PROBE_COLS],
+            zeros[:, 0:1].to_broadcast([P, P]),
+            base_tile[:, 0:PROBE_COLS],
+            start=True,
+            stop=True,
+        )
 
         for e in range(E):
             places = window[:].indirect(offsets[:, e * QC : (e + 1) * QC])

import concourse.mybir as mybir
from concourse.masks import make_identity

P = 128
S = 512
K = 256
N = 384
E = 4
Q = N // E
KB = K // P
QC = Q // 16
HEAD = 512
EARLY = (HEAD - (KB - 1) * N) // Q

WARM_UPS = 3
WARM_COLS = 512
ZERO_COLS = 16
HALVES = 2
PROBE_COLS = 256
ALIGN = 256

FLOPS = 2 * K * P * N

BF16, F32, U16 = mybir.dt.bfloat16, mybir.dt.float32, mybir.dt.uint16


def tile_scatter_matmul_kernel(tc, base, x, w, b, offs, out):
    nc = tc.nc
    with (
        tc.tile_pool(name="held", bufs=1) as held,
        tc.psum_pool(name="psum", bufs=1) as psum,
    ):
        offsets = held.tile([P, N // 16], U16, name="offsets")
        nc.sync.dma_start(offsets[:], offs)
        bias = held.tile([P, 1], F32, name="bias")
        nc.sync.dma_start(bias[:], b)

        zeros = held.tile([P, ZERO_COLS], BF16, name="zeros")
        nc.gpsimd.memset(zeros[:], 0.0)
        unread = psum.tile([P, WARM_COLS], F32, name="unread")
        for i in range(WARM_UPS):
            nc.tensor.matmul(
                unread[:],
                zeros[:, 0:1].to_broadcast([P, P]),
                zeros[:, 0:1].to_broadcast([P, WARM_COLS]),
                start=True,
                stop=True,
            )

        ident = held.tile([P, P], BF16, name="ident")
        make_identity(nc, ident[:])

        base_tile = held.tile([P, S], BF16, name="base_tile", align_bytes=ALIGN)
        nc.scalar.dma_start(base_tile[:], base)

        x_runs = x.rearrange("(p a) n -> p (a n)", a=KB)
        x_tile = held.tile([P, KB * N], BF16, name="x_tile", align_bytes=ALIGN)
        nc.scalar.dma_start(x_tile[:, 0:HEAD], x_runs[:, 0:HEAD])

        w_tiles = []
        for e in range(E):
            w_tile = held.tile([P, KB, P], BF16, name="w_tile%d" % e, align_bytes=ALIGN)
            nc.scalar.dma_start(w_tile[:], w[e].rearrange("(p a) m -> p a m", a=KB))
            w_tiles.append(w_tile)
            if e == EARLY:
                nc.scalar.dma_start(x_tile[:, HEAD : KB * N], x_runs[:, HEAD : KB * N])

        window = psum.tile([P, S], F32, name="window")
        nc.tensor.matmul(window[:], ident[:], base_tile[:], start=True, stop=False)

        nc.tensor.matmul(
            unread[:, 0:PROBE_COLS],
            zeros[:, 0:1].to_broadcast([P, P]),
            base_tile[:, 0:PROBE_COLS],
            start=True,
            stop=True,
        )

        for e in range(E):
            places = window[:].indirect(offsets[:, e * QC : (e + 1) * QC])
            for a in range(KB):
                first = a * N + e * Q
                nc.tensor.matmul(
                    places,
                    w_tiles[e][:, a, :],
                    x_tile[:, first : first + Q],
                    start=False,
                    stop=(e == E - 1 and a == KB - 1),
                )

        for h in range(HALVES):
            cols = slice(h * S // HALVES, (h + 1) * S // HALVES)
            result = held.tile([P, S // HALVES], F32, name="result%d" % h, align_bytes=ALIGN)
            nc.vector.tensor_scalar_add(result[:], window[:, cols], bias[:])
            nc.sync.dma_start(out[:, cols], result[:])
